import numpy as np
CORES = [44,45,46,47,172,173,174,175,300,301,302,303,428,429,430,431]
N = 16
C = 512
def setup_inputs(rng):
    return {"x": rng.standard_normal((N, 128, C), dtype=np.float32)}
def setup_inputs_big(rng):
    d = setup_inputs(rng)
    for k in ("x",): d[k] = (d[k].astype(np.float32) * 1048576.0).astype(d[k].dtype)
    return d
def setup_inputs_small(rng):
    d = setup_inputs(rng)
    for k in ("x",): d[k] = (d[k].astype(np.float32) * (1 / 1048576.0)).astype(d[k].dtype)
    return d
def setup_inputs_apart(rng):
    d = setup_inputs(rng)
    f = (10.0 ** rng.permutation(np.linspace(-1.5, 1.5, N))).astype(np.float32).reshape(N, 1, 1)
    for k in ("x",): d[k] = (d[k].astype(np.float32) * f).astype(d[k].dtype)
    return d
def reference(x):
    X = x.astype(np.float64)
    y = np.stack([sum(np.maximum(X[r] - X[s], 0.0) for s in range(N)) for r in range(N)])
    return {"y": y.astype(np.float32)}

@@ -1,0 +1,286 @@
+from concourse.bass import DstId, RemoteDMATransfer
+from concourse.mybir import AluOpType
+
+B, Q, H, C = 64, 128, 256, 512
+
+SCRATCH = {
+    "xs": ("sbuf", [128, C], "float32"),
+    "c15": ("sbuf", [128, C], "float32"),
+    "wl": ("sbuf", [128, 4 * B], "float32"),
+    "ll": ("sbuf", [128, 4 * B], "float32"),
+    "rl": ("sbuf", [128, 4 * B], "float32"),
+    "m1": ("sbuf", [128, 3 * H], "float32"),
+    "m2": ("sbuf", [128, 3 * H], "float32"),
+    "part": ("sbuf", [128, H], "float32"),
+    "resL": ("sbuf", [128, H], "float32"),
+    "resR": ("sbuf", [128, H], "float32"),
+    "resW": ("sbuf", [128, H], "float32"),
+    "sw": ("sbuf", [128, 4 * H], "float32"),
+    "resS": ("sbuf", [128, 4 * H], "float32"),
+    "lS": ("sbuf", [128, C], "float32"),
+    "lO": ("sbuf", [128, C], "float32"),
+    "lA": ("sbuf", [128, C], "float32"),
+    "lB": ("sbuf", [128, C], "float32"),
+    "out": ("sbuf", [128, C], "float32"),
+    "wwp": ("psum", [128, C], "float32"),
+    "llp": ("psum", [128, C], "float32"),
+    "pm": ("psum", [128, C], "float32"),
+    "t1": ("psum", [128, C], "float32"),
+    "t2": ("psum", [128, C], "float32"),
+    "u": ("psum", [128, C], "float32"),
+}
+SEMAPHORES = ["sLd", "sL", "sR", "sW", "sS", "sE", "sX", "sM", "sF", "sLoc", "dv", "st0", "st1"]
+
+
+def _plan(T, topo):
+    hosts = []
+    for c in T.cores:
+        if topo.host(c) not in hosts:
+            hosts.append(topo.host(c))
+    by = {h: [c for c in T.cores if topo.host(c) == h] for h in hosts}
+    ring = [hosts[0]]
+    while len(ring) < len(hosts):
+        ring.append([h for h in hosts if h not in ring and topo.may_write(by[ring[-1]][0], by[h][0])][0])
+    n = len(ring)
+    ranks = [by[h] for h in ring]
+    world = range((max(hosts) + 1) * topo.CORES_PER_HOST)
+    SW, CW, role = [], [], {}
+    for p in range(n):
+        r = ranks[p]
+        helpers = [c for c in world if topo.host(c) == ring[p] and topo.chip(c) == topo.chip(r[0]) and c not in r]
+        SW.append([r[0], r[1]])
+        CW.append({1: [r[2], r[3]], 2: helpers[0:2], 3: helpers[2:4]})
+        for q in (0, 1):
+            role[SW[p][q]] = {"p": p, "kind": "self", "q": q}
+        for d in (1, 2, 3):
+            for hb in (0, 1):
+                role[CW[p][d][hb]] = {"p": p, "kind": "cross", "d": d, "hb": hb}
+        for i in range(4):
+            role[r[i]]["i"] = i
+    sends = {}
+    for p in range(n):
+        rt, lf = (p + 1) % n, (p - 1) % n
+        for i, c in enumerate(ranks[p]):
+            F1, F3, FW, FS = [], [], [], []
+            sl = (i * B, (i + 1) * B)
+            for d in (1, 2, 3):
+                for hb in (0, 1):
+                    b = (2 * ((rt + d) % n) + hb) * B
+                    F1.append((CW[rt][d][hb], ("ll",) + sl, ("xs", b, b + B), 1, "off", "sL"))
+            for d in (1, 2, 3):
+                for hb in (0, 1):
+                    b = (2 * ((lf + d) % n) + hb) * B
+                    (F1 if d == 1 else F3).append(
+                        (CW[lf][d][hb], ("rl",) + sl, ("xs", b, b + B), 1 if d == 1 else 2, "off", "sR"))
+                    b = (2 * ((p + d) % n) + hb) * B
+                    if CW[p][d][hb] != c:
+                        FW.append((CW[p][d][hb], ("wl",) + sl, ("xs", b, b + B), 1, "hi", "sW"))
+            for q in (0, 1):
+                if SW[p][q] != c:
+                    FS.append((SW[p][q], ("sw", i * H, (i + 1) * H), ("xs", q * H, (q + 1) * H), 4, "hi", "sS"))
+            sends[(c, "F1")], sends[(c, "FW")], sends[(c, "F3")], sends[(c, "FS")] = F1, FW, F3, FS
+        for d in (1, 2, 3):
+            for hb in (0, 1):
+                c = CW[p][d][hb]
+                b = (2 * ((p + d) % n) + hb) * B
+                far = "lB" if d == 1 else "lA"
+                sends[(c, "RL")] = [(ranks[lf][i], (far, b, b + B), ("resL", i * B, (i + 1) * B), 2, "off",
+                                     "sE" if d == 1 else "sF") for i in range(4)]
+                sends[(c, "RR")] = [(ranks[rt][i], (far, b, b + B), ("resR", i * B, (i + 1) * B), 2, "off",
+                                     "sM" if d == 1 else "sF") for i in range(4)]
+                sends[(c, "RW")] = [(ranks[p][i], ("lO", b, b + B), ("resW", i * B, (i + 1) * B), 2,
+                                     "hi" if d == 1 else "off", "sM" if d == 1 else "sE")
+                                    for i in range(4) if ranks[p][i] != c]
+        for q in (0, 1):
+            c = SW[p][q]
+            sends[(c, "RS")] = [(ranks[p][i], ("lS", q * H, (q + 1) * H), ("resS", i * H, (i + 1) * H), 4, "on", "sX")
+                                for i in range(4) if ranks[p][i] != c]
+    expect = {}
+    for key in sends:
+        for t in sends[key]:
+            expect[(t[0], t[5])] = expect.get((t[0], t[5]), 0) + t[3]
+    return role, sends, expect, ranks, SW, CW, n
+
+
+def rank_program(g, core, T, topo):
+    if not [c for c in T.cores if topo.host(c) == topo.host(core) and topo.chip(c) == topo.chip(core)]:
+        return
+    role, sends, expect, ranks, SW, CW, n = _plan(T, topo)
+    me = role[core]
+    p = me["p"]
+    i = me.get("i")
+    v = g.vector
+    sem = T.sem
+
+    def ap(o):
+        return T[o[0]][:, o[1]:o[2]]
+
+    def bits(m):
+        return [1 << e for e in range(16) if (m >> e) & 1]
+    off = bits(topo.mask(core, ranks[(p + 1) % n][0]))
+    on = bits(topo.mask(core, [c for c in role if role[c]["p"] == p and c != core][0]))
+    pools = {"off": off, "on": on, "hi": [e for e in on if e not in off]}
+    loc = [0]
+
+    def call(key):
+        used = {"off": 0, "on": 0, "hi": 0}
+        trs = []
+        for (dst, d_, s_, ne, pool, sm) in sends[(core, key)]:
+            m = sum(pools[pool][used[pool]:used[pool] + ne])
+            used[pool] += ne
+            rid, pid = topo.addr(dst, core)
+            trs.append(RemoteDMATransfer(dst_ids=[DstId(rid=rid, pnc=pid)], dma_engine_mask=m, remote_sem=sem[sm],
+                                         src=ap(s_), dst=ap(d_)))
+            loc[0] += ne
+        g.remote_dma_fused(trs, local_sem=sem.sLoc)
+
+    st = {"n": 0, "w": 0}
+    lastw, lastr = {}, {}
+
+    def keys(o):
+        return [(o[0], k) for k in range(o[1] // B, (o[2] + B - 1) // B)]
+
+    def dep(reads, out):
+        need = 0
+        for o in reads + [out]:
+            for k in keys(o):
+                need = max(need, lastw.get(k, 0))
+        for k in keys(out):
+            need = max(need, lastr.get(k, 0))
+        if need > st["w"]:
+            v.wait_ge(sem.dv, need)
+            st["w"] = need
+        st["n"] += 1
+        for o in reads:
+            for k in keys(o):
+                lastr[k] = st["n"]
+        for k in keys(out):
+            lastw[k] = st["n"]
+
+    def tt(out, a, b, op):
+        dep([a, b], out)
+        v.tensor_tensor(out=ap(out), in0=ap(a), in1=ap(b), op=op).then_inc(sem.dv, 1)
+
+    def cp(out, a):
+        dep([a], out)
+        v.tensor_copy(out=ap(out), in_=ap(a)).then_inc(sem.dv, 1)
+
+    def vwait(name):
+        if expect.get((core, name), 0):
+            v.wait_ge(sem[name], expect[(core, name)])
+
+    def sub(o, a, b):
+        return (o[0], o[1] + a * B, o[1] + b * B)
+
+    ADD, MIN, SUBT = AluOpType.add, AluOpType.min, AluOpType.subtract
+
+    def mins(A, Bp, M):
+        for k in range(4):
+            tt(M[k], (A, 0, H), (Bp, k * B, k * B + H), MIN)
+
+    def sum_a(M, t, res):
+        for k in (1, 2, 3):
+            for h in (0, 2):
+                tt(sub(res if k == 3 else t, h, h + 2), sub(M[0] if k == 1 else t, h, h + 2), sub(M[k], h, h + 2), ADD)
+
+    def sum_b(M, t, res, part):
+        if part:
+            tt(t, M[0], part, ADD)
+        for k in (1, 2, 3):
+            base = M[0] if (k == 1 and not part) else t
+            o = res if k == 3 else t
+            tt(sub(o, k, 4), sub(base, k, 4), sub(M[k], 0, 4 - k), ADD)
+            tt(sub(o, 0, k), sub(base, 0, k), sub(M[k], 4 - k, 4), ADD)
+
+    marks = []
+
+    if i is not None:
+        g.sync.dma_start(T.xs[:], T.x[:]).then_inc(sem.sLd, 16)
+        dep([], ("c15", 0, C))
+        v.memset(T.c15[:], float(len(T.cores) - 1)).then_inc(sem.dv, 1)
+        v.wait_ge(sem.sLd, 16)
+        tt(("u", 0, C), ("xs", 0, C), ("c15", 0, C), AluOpType.mult)
+
+    if me["kind"] == "self":
+        q = me["q"]
+        s = [("sw", a * H, (a + 1) * H) if a != i else ("xs", q * H, (q + 1) * H) for a in range(4)]
+        sp = [None, ("wwp", 0, H), ("wwp", H, C), ("llp", 0, H)]
+        vwait("sS")
+        for a in (1, 2, 3):
+            cp(sp[a], s[a])
+        m = {(0, 1): ("pm", 0, H), (2, 3): ("pm", H, C), (0, 2): ("m1", 0, H), (0, 3): ("m1", H, 2 * H),
+             (1, 2): ("m1", 2 * H, 3 * H), (1, 3): ("m2", 0, H)}
+        for (a, b) in ((0, 1), (2, 3), (0, 2), (0, 3), (1, 2), (1, 3)):
+            tt(m[(a, b)], s[a], sp[b], MIN)
+        tq = [("t1", 0, H), ("t1", H, C), ("t2", 0, H), ("t2", H, C)]
+        terms = [((0, 1), (0, 2), (0, 3)), ((0, 1), (1, 2), (1, 3)), ((2, 3), (0, 2), (1, 2)), ((2, 3), (0, 3), (1, 3))]
+        for a in range(4):
+            tt(tq[a], m[terms[a][0]], m[terms[a][1]], ADD)
+        for a in range(4):
+            tt(("resS", a * H, (a + 1) * H), tq[a], m[terms[a][2]], ADD)
+        marks.append(("RS", st["n"]))
+    else:
+        d, hb = me["d"], me["hb"]
+        b0 = (2 * ((p + d) % n) + hb) * B
+        vwait("sW")
+        if i is None:
+            cp(("wwp", 0, H), ("wl", 0, H))
+            cp(("wwp", H, H + 3 * B), ("wl", 0, 3 * B))
+        else:
+            for a in range(7):
+                cp(("wwp", a * B, (a + 1) * B), ("wl", (a % 4) * B, (a % 4 + 1) * B) if a % 4 != i else ("xs", b0, b0 + B))
+        M1 = [("pm", 0, H)] + [("m1", k * H, (k + 1) * H) for k in range(3)]
+        M2 = [("pm", H, C)] + [("m2", k * H, (k + 1) * H) for k in range(3)]
+        vwait("sL")
+        mins("ll", "wwp", M1)
+        if d == 1:
+            sum_a(M1, ("t1", 0, H), ("resL", 0, H))
+            marks.append(("RL", st["n"]))
+            sum_b(M1, ("t1", H, C), ("part", 0, H), None)
+        else:
+            sum_b(M1, ("t1", H, C), ("resW", 0, H), None)
+            marks.append(("RW", st["n"]))
+            sum_a(M1, ("t1", 0, H), ("part", 0, H))
+            cp(("llp", 0, H), ("ll", 0, H))
+            cp(("llp", H, H + 3 * B), ("ll", 0, 3 * B))
+        vwait("sR")
+        mins("rl", "wwp" if d == 1 else "llp", M2)
+        sum_a(M2, ("t2", 0, H), ("resR", 0, H))
+        marks.append(("RR", st["n"]))
+        sum_b(M2, ("t2", H, C), ("resW", 0, H) if d == 1 else ("resL", 0, H), ("part", 0, H))
+        marks.append(("RW" if d == 1 else "RL", st["n"]))
+
+    if i is not None:
+        def col(dd):
+            return ((p + dd) % n) * Q
+
+        def less(c0, c1, src, o="u"):
+            tt((o, c0, c1), ("u", c0, c1), src, SUBT)
+        vwait("sE")
+        for dd in (3, 2):
+            less(col(dd), col(dd) + Q, ("lO", col(dd), col(dd) + Q))
+        less(col(2), col(2) + Q, ("lB", col(2), col(2) + Q))
+        vwait("sX")
+        for q in (0, 1):
+            less(q * H, (q + 1) * H, ("resS", i * H, (i + 1) * H) if SW[p][q] == core else ("lS", q * H, (q + 1) * H))
+        vwait("sM")
+        for hb in (0, 1):
+            c0 = col(1) + hb * B
+            less(c0, c0 + B, ("resW", i * B, (i + 1) * B) if CW[p][1][hb] == core else ("lO", c0, c0 + B))
+        less(col(0), col(0) + Q, ("lB", col(0), col(0) + Q))
+        vwait("sF")
+        for q, eng, s_ in ((0, g.sync, sem.st0), (1, g.scalar, sem.st1)):
+            less(q * H, (q + 1) * H, ("lA", q * H, (q + 1) * H), "out")
+            eng.wait_ge(sem.dv, st["n"])
+            eng.dma_start(T.y[:, q * H:(q + 1) * H], T.out[:, q * H:(q + 1) * H]).then_inc(s_, 16)
+            eng.wait_ge(s_, 16)
+
+    if i is not None:
+        g.wait_ge(sem.sLd, 16)
+        for key in ("F1", "FW", "F3", "FS"):
+            call(key)
+    for key, cnt in marks:
+        g.wait_ge(sem.dv, cnt)
+        call(key)
+    g.wait_ge(sem.sLoc, loc[0])
+    g.wait_ge(sem.dv, st["n"])

@@ -6,30 +6,34 @@ B, Q, H, C = 64, 128, 256, 512
 SCRATCH = {
     "xs": ("sbuf", [128, C], "float32"),
     "c15": ("sbuf", [128, C], "float32"),
-    "wl": ("sbuf", [128, 4 * B], "float32"),
-    "ll": ("sbuf", [128, 4 * B], "float32"),
-    "rl": ("sbuf", [128, 4 * B], "float32"),
+    "wl": ("sbuf", [128, H], "float32"),
+    "wl0": ("sbuf", [128, H], "float32"),
+    "ll": ("sbuf", [128, H], "float32"),
+    "rl": ("sbuf", [128, H], "float32"),
+    "sc": ("sbuf", [128, 6 * B], "float32"),
+    "sc0": ("sbuf", [128, 6 * B], "float32"),
+    "ssum": ("sbuf", [128, H], "float32"),
     "m1": ("sbuf", [128, 3 * H], "float32"),
     "m2": ("sbuf", [128, 3 * H], "float32"),
     "part": ("sbuf", [128, H], "float32"),
+    "res0": ("sbuf", [128, H], "float32"),
     "resL": ("sbuf", [128, H], "float32"),
     "resR": ("sbuf", [128, H], "float32"),
     "resW": ("sbuf", [128, H], "float32"),
-    "sw": ("sbuf", [128, 4 * H], "float32"),
-    "resS": ("sbuf", [128, 4 * H], "float32"),
-    "lS": ("sbuf", [128, C], "float32"),
     "lO": ("sbuf", [128, C], "float32"),
     "lA": ("sbuf", [128, C], "float32"),
     "lB": ("sbuf", [128, C], "float32"),
+    "lC": ("sbuf", [128, C], "float32"),
     "out": ("sbuf", [128, C], "float32"),
     "wwp": ("psum", [128, C], "float32"),
     "llp": ("psum", [128, C], "float32"),
     "pm": ("psum", [128, C], "float32"),
+    "ts": ("psum", [128, C], "float32"),
     "t1": ("psum", [128, C], "float32"),
     "t2": ("psum", [128, C], "float32"),
     "u": ("psum", [128, C], "float32"),
 }
-SEMAPHORES = ["sLd", "sL", "sR", "sW", "sS", "sE", "sX", "sM", "sF", "sLoc", "dv", "st0", "st1"]
+SEMAPHORES = ["sLd", "sL", "sR", "sW", "sW0", "sE", "sF", "sG", "sM", "sLoc", "dv", "st0", "st1"]
 
 
 def _plan(T, topo):
@@ -44,70 +48,71 @@ def _plan(T, topo):
     n = len(ring)
     ranks = [by[h] for h in ring]
     world = range((max(hosts) + 1) * topo.CORES_PER_HOST)
-    SW, CW, role = [], [], {}
+    CW, role = [], {}
     for p in range(n):
         r = ranks[p]
-        helpers = [c for c in world if topo.host(c) == ring[p] and topo.chip(c) == topo.chip(r[0]) and c not in r]
-        SW.append([r[0], r[1]])
-        CW.append({1: [r[2], r[3]], 2: helpers[0:2], 3: helpers[2:4]})
-        for q in (0, 1):
-            role[SW[p][q]] = {"p": p, "kind": "self", "q": q}
-        for d in (1, 2, 3):
+        others = [c for c in world if topo.host(c) == ring[p] and topo.chip(c) == topo.chip(r[0]) and c not in r]
+        CW.append({"LW": r[0:2], "RW": r[2:4], 2: others[0:2], 3: others[2:4]})
+        for k in CW[p]:
             for hb in (0, 1):
-                role[CW[p][d][hb]] = {"p": p, "kind": "cross", "d": d, "hb": hb}
+                role[CW[p][k][hb]] = {"p": p, "k": k, "hb": hb}
         for i in range(4):
             role[r[i]]["i"] = i
     sends = {}
     for p in range(n):
         rt, lf = (p + 1) % n, (p - 1) % n
+
+        def blk(q, d, hb):
+            return (2 * ((q + d) % n) + hb) * B
+
+        def sl(name, i):
+            return (name, i * B, (i + 1) * B)
+
+        def xb(b):
+            return ("xs", b, b + B)
         for i, c in enumerate(ranks[p]):
-            F1, F3, FW, FS = [], [], [], []
-            sl = (i * B, (i + 1) * B)
-            for d in (1, 2, 3):
-                for hb in (0, 1):
-                    b = (2 * ((rt + d) % n) + hb) * B
-                    F1.append((CW[rt][d][hb], ("ll",) + sl, ("xs", b, b + B), 1, "off", "sL"))
-            for d in (1, 2, 3):
-                for hb in (0, 1):
-                    b = (2 * ((lf + d) % n) + hb) * B
-                    (F1 if d == 1 else F3).append(
-                        (CW[lf][d][hb], ("rl",) + sl, ("xs", b, b + B), 1 if d == 1 else 2, "off", "sR"))
-                    b = (2 * ((p + d) % n) + hb) * B
-                    if CW[p][d][hb] != c:
-                        FW.append((CW[p][d][hb], ("wl",) + sl, ("xs", b, b + B), 1, "hi", "sW"))
-            for q in (0, 1):
-                if SW[p][q] != c:
-                    FS.append((SW[p][q], ("sw", i * H, (i + 1) * H), ("xs", q * H, (q + 1) * H), 4, "hi", "sS"))
-            sends[(c, "F1")], sends[(c, "FW")], sends[(c, "F3")], sends[(c, "FS")] = F1, FW, F3, FS
-        for d in (1, 2, 3):
+            F = {"C1": [], "C2": [], "C3": []}
             for hb in (0, 1):
-                c = CW[p][d][hb]
-                b = (2 * ((p + d) % n) + hb) * B
-                far = "lB" if d == 1 else "lA"
-                sends[(c, "RL")] = [(ranks[lf][i], (far, b, b + B), ("resL", i * B, (i + 1) * B), 2, "off",
-                                     "sE" if d == 1 else "sF") for i in range(4)]
-                sends[(c, "RR")] = [(ranks[rt][i], (far, b, b + B), ("resR", i * B, (i + 1) * B), 2, "off",
-                                     "sM" if d == 1 else "sF") for i in range(4)]
-                sends[(c, "RW")] = [(ranks[p][i], ("lO", b, b + B), ("resW", i * B, (i + 1) * B), 2,
-                                     "hi" if d == 1 else "off", "sM" if d == 1 else "sE")
-                                    for i in range(4) if ranks[p][i] != c]
-        for q in (0, 1):
-            c = SW[p][q]
-            sends[(c, "RS")] = [(ranks[p][i], ("lS", q * H, (q + 1) * H), ("resS", i * H, (i + 1) * H), 4, "on", "sX")
-                                for i in range(4) if ranks[p][i] != c]
+                for d in (2, 3):
+                    F["C1"].append((CW[rt][d][hb], sl("ll", i), xb(blk(rt, d, hb)), 1, "off", "sL"))
+                    F["C1"].append((CW[lf][d][hb], sl("rl", i), xb(blk(lf, d, hb)), 1, "off", "sR"))
+                    F["C1"].append((CW[p][d][hb], sl("wl", i), xb(blk(p, d, hb)), 2, "hi", "sW"))
+                F["C2"].append((CW[rt]["LW"][hb], sl("ll", i), xb(blk(rt, 1, hb)), 2, "off", "sL"))
+                F["C2"].append((CW[lf]["RW"][hb], sl("rl", i), xb(blk(lf, 1, hb)), 2, "off", "sR"))
+                F["C2"].append((CW[p]["LW"][hb], sl("wl", i), xb(blk(p, 1, hb)), 2, "hi", "sW"))
+                F["C2"].append((CW[p]["RW"][hb], sl("wl", i), xb(blk(p, 1, hb)), 2, "hi", "sW"))
+                F["C3"].append((CW[p]["LW"][hb], sl("wl0", i), xb(blk(p, 0, hb)), 4, "hi", "sW0"))
+            for key in F:
+                sends[(c, key)] = [t for t in F[key] if t[0] != c]
+
+        def ret(c, key, to, land, b, res, pool, sm):
+            sends[(c, key)] = sends.get((c, key), []) + [
+                (to[i], (land, b, b + B), sl(res, i), 2, pool, sm) for i in range(4) if to[i] != c]
+        for hb in (0, 1):
+            for d in (2, 3):
+                c, b = CW[p][d][hb], blk(p, d, hb)
+                ret(c, "RR", ranks[rt], "lA", b, "resR", "off", "sF")
+                ret(c, "RX", ranks[lf], "lA", b, "resL", "off", "sG")
+                ret(c, "RX", ranks[p], "lO", b, "resW", "hi", "sG")
+            b = blk(p, 1, hb)
+            ret(CW[p]["LW"][hb], "R0", ranks[p], "lO", blk(p, 0, hb), "res0", "hi", "sE")
+            ret(CW[p]["LW"][hb], "RX", ranks[lf], "lB", b, "resL", "off", "sM")
+            ret(CW[p]["LW"][hb], "RX", ranks[p], "lO", b, "resW", "hi", "sM")
+            ret(CW[p]["RW"][hb], "RX", ranks[rt], "lB", b, "resR", "off", "sM")
+            ret(CW[p]["RW"][hb], "RX", ranks[p], "lC", b, "resW", "hi", "sM")
     expect = {}
     for key in sends:
         for t in sends[key]:
             expect[(t[0], t[5])] = expect.get((t[0], t[5]), 0) + t[3]
-    return role, sends, expect, ranks, SW, CW, n
+    return role, sends, expect, ranks, CW, n
 
 
 def rank_program(g, core, T, topo):
     if not [c for c in T.cores if topo.host(c) == topo.host(core) and topo.chip(c) == topo.chip(core)]:
         return
-    role, sends, expect, ranks, SW, CW, n = _plan(T, topo)
+    role, sends, expect, ranks, CW, n = _plan(T, topo)
     me = role[core]
-    p = me["p"]
+    p, kind, hb = me["p"], me["k"], me["hb"]
     i = me.get("i")
     v = g.vector
     sem = T.sem
@@ -119,11 +124,11 @@ def rank_program(g, core, T, topo):
         return [1 << e for e in range(16) if (m >> e) & 1]
     off = bits(topo.mask(core, ranks[(p + 1) % n][0]))
     on = bits(topo.mask(core, [c for c in role if role[c]["p"] == p and c != core][0]))
-    pools = {"off": off, "on": on, "hi": [e for e in on if e not in off]}
+    pools = {"off": off, "hi": [e for e in on if e not in off]}
     loc = [0]
 
     def call(key):
-        used = {"off": 0, "on": 0, "hi": 0}
+        used = {"off": 0, "hi": 0}
         trs = []
         for (dst, d_, s_, ne, pool, sm) in sends[(core, key)]:
             m = sum(pools[pool][used[pool]:used[pool] + ne])
@@ -174,6 +179,19 @@ def rank_program(g, core, T, topo):
 
     ADD, MIN, SUBT = AluOpType.add, AluOpType.min, AluOpType.subtract
 
+    def wide(dst, src):
+        cp((dst, 0, H), (src, 0, H))
+        cp((dst, H, H + 3 * B), (src, 0, 3 * B))
+
+    def inside(w, wp, s, ts, ss):
+        c1, c2 = (s, 0, H), (s, H, H + 2 * B)
+        tt(c1, (w, 0, H), (wp, B, B + H), MIN)
+        tt(c2, (w, 0, 2 * B), (wp, 2 * B, 4 * B), MIN)
+        tt(sub(ts, 1, 4), sub(c1, 1, 4), sub(c1, 0, 3), ADD)
+        tt(sub(ts, 0, 1), sub(c1, 0, 1), sub(c1, 3, 4), ADD)
+        tt(sub(ss, 2, 4), sub(ts, 2, 4), c2, ADD)
+        tt(sub(ss, 0, 2), sub(ts, 0, 2), c2, ADD)
+
     def mins(A, Bp, M):
         for k in range(4):
             tt(M[k], (A, 0, H), (Bp, k * B, k * B + H), MIN)
@@ -194,90 +212,100 @@ def rank_program(g, core, T, topo):
 
     marks = []
 
+    def mark(key):
+        marks.append((key, st["n"]))
+
+    def col(dd):
+        return ((p + dd) % n) * Q
+
+    M1 = [("pm", 0, H)] + [("m1", k * H, (k + 1) * H) for k in range(3)]
+    M2 = [("pm", H, C)] + [("m2", k * H, (k + 1) * H) for k in range(3)]
+    ss = ("ssum", 0, H)
+
     if i is not None:
         g.sync.dma_start(T.xs[:], T.x[:]).then_inc(sem.sLd, 16)
         dep([], ("c15", 0, C))
         v.memset(T.c15[:], float(len(T.cores) - 1)).then_inc(sem.dv, 1)
         v.wait_ge(sem.sLd, 16)
+        b1 = col(1) + hb * B
+        cp(("wl", i * B, (i + 1) * B), ("xs", b1, b1 + B))
+        if kind == "LW":
+            cp(("wl0", i * B, (i + 1) * B), ("xs", col(0) + hb * B, col(0) + hb * B + B))
         tt(("u", 0, C), ("xs", 0, C), ("c15", 0, C), AluOpType.mult)
 
-    if me["kind"] == "self":
-        q = me["q"]
-        s = [("sw", a * H, (a + 1) * H) if a != i else ("xs", q * H, (q + 1) * H) for a in range(4)]
-        sp = [None, ("wwp", 0, H), ("wwp", H, C), ("llp", 0, H)]
-        vwait("sS")
-        for a in (1, 2, 3):
-            cp(sp[a], s[a])
-        m = {(0, 1): ("pm", 0, H), (2, 3): ("pm", H, C), (0, 2): ("m1", 0, H), (0, 3): ("m1", H, 2 * H),
-             (1, 2): ("m1", 2 * H, 3 * H), (1, 3): ("m2", 0, H)}
-        for (a, b) in ((0, 1), (2, 3), (0, 2), (0, 3), (1, 2), (1, 3)):
-            tt(m[(a, b)], s[a], sp[b], MIN)
-        tq = [("t1", 0, H), ("t1", H, C), ("t2", 0, H), ("t2", H, C)]
-        terms = [((0, 1), (0, 2), (0, 3)), ((0, 1), (1, 2), (1, 3)), ((2, 3), (0, 2), (1, 2)), ((2, 3), (0, 3), (1, 3))]
-        for a in range(4):
-            tt(tq[a], m[terms[a][0]], m[terms[a][1]], ADD)
-        for a in range(4):
-            tt(("resS", a * H, (a + 1) * H), tq[a], m[terms[a][2]], ADD)
-        marks.append(("RS", st["n"]))
-    else:
-        d, hb = me["d"], me["hb"]
-        b0 = (2 * ((p + d) % n) + hb) * B
+    if kind == "LW":
         vwait("sW")
-        if i is None:
-            cp(("wwp", 0, H), ("wl", 0, H))
-            cp(("wwp", H, H + 3 * B), ("wl", 0, 3 * B))
-        else:
-            for a in range(7):
-                cp(("wwp", a * B, (a + 1) * B), ("wl", (a % 4) * B, (a % 4 + 1) * B) if a % 4 != i else ("xs", b0, b0 + B))
-        M1 = [("pm", 0, H)] + [("m1", k * H, (k + 1) * H) for k in range(3)]
-        M2 = [("pm", H, C)] + [("m2", k * H, (k + 1) * H) for k in range(3)]
+        wide("wwp", "wl")
+        inside("wl", "wwp", "sc", ("ts", 0, H), ss)
+        vwait("sW0")
+        wide("llp", "wl0")
+        inside("wl0", "llp", "sc0", ("ts", H, C), ("res0", 0, H))
+        mark("R0")
         vwait("sL")
         mins("ll", "wwp", M1)
-        if d == 1:
-            sum_a(M1, ("t1", 0, H), ("resL", 0, H))
-            marks.append(("RL", st["n"]))
-            sum_b(M1, ("t1", H, C), ("part", 0, H), None)
-        else:
-            sum_b(M1, ("t1", H, C), ("resW", 0, H), None)
-            marks.append(("RW", st["n"]))
-            sum_a(M1, ("t1", 0, H), ("part", 0, H))
-            cp(("llp", 0, H), ("ll", 0, H))
-            cp(("llp", H, H + 3 * B), ("ll", 0, 3 * B))
+        sum_a(M1, ("t1", 0, H), ("resL", 0, H))
+        sum_b(M1, ("t1", H, C), ("resW", 0, H), ss)
+        mark("RX")
+    elif kind == "RW":
+        vwait("sW")
+        wide("wwp", "wl")
         vwait("sR")
-        mins("rl", "wwp" if d == 1 else "llp", M2)
+        mins("rl", "wwp", M2)
         sum_a(M2, ("t2", 0, H), ("resR", 0, H))
-        marks.append(("RR", st["n"]))
-        sum_b(M2, ("t2", H, C), ("resW", 0, H) if d == 1 else ("resL", 0, H), ("part", 0, H))
-        marks.append(("RW" if d == 1 else "RL", st["n"]))
+        sum_b(M2, ("t2", H, C), ("resW", 0, H), None)
+        mark("RX")
+    else:
+        vwait("sW")
+        wide("wwp", "wl")
+        inside("wl", "wwp", "sc", ("ts", 0, H), ss)
+        vwait("sL")
+        wide("llp", "ll")
+        vwait("sR")
+        mins("rl", "llp", M2)
+        sum_a(M2, ("t2", 0, H), ("resR", 0, H))
+        mark("RR")
+        mins("ll", "wwp", M1)
+        sum_b(M1, ("t1", H, C), ("resW", 0, H), ss)
+        sum_a(M1, ("t1", 0, H), ("part", 0, H))
+        sum_b(M2, ("t2", H, C), ("resL", 0, H), ("part", 0, H))
+        mark("RX")
 
     if i is not None:
-        def col(dd):
-            return ((p + dd) % n) * Q
+        done = {}
 
-        def less(c0, c1, src, o="u"):
-            tt((o, c0, c1), ("u", c0, c1), src, SUBT)
+        def less(dd, land, o="u", makers=None, res=None):
+            if makers and core in makers:
+                for h in (0, 1):
+                    c0 = col(dd) + h * B
+                    tt((o, c0, c0 + B), ("u", c0, c0 + B),
+                       (res, i * B, (i + 1) * B) if makers[h] == core else (land, c0, c0 + B), SUBT)
+            else:
+                tt((o, col(dd), col(dd) + Q), ("u", col(dd), col(dd) + Q), (land, col(dd), col(dd) + Q), SUBT)
+            if o == "out":
+                done[col(dd) // H] = st["n"]
         vwait("sE")
-        for dd in (3, 2):
-            less(col(dd), col(dd) + Q, ("lO", col(dd), col(dd) + Q))
-        less(col(2), col(2) + Q, ("lB", col(2), col(2) + Q))
-        vwait("sX")
-        for q in (0, 1):
-            less(q * H, (q + 1) * H, ("resS", i * H, (i + 1) * H) if SW[p][q] == core else ("lS", q * H, (q + 1) * H))
-        vwait("sM")
-        for hb in (0, 1):
-            c0 = col(1) + hb * B
-            less(c0, c0 + B, ("resW", i * B, (i + 1) * B) if CW[p][1][hb] == core else ("lO", c0, c0 + B))
-        less(col(0), col(0) + Q, ("lB", col(0), col(0) + Q))
+        less(0, "lO", "u", CW[p]["LW"], "res0")
         vwait("sF")
+        less(1, "lA")
+        less(2, "lA")
+        vwait("sG")
+        less(3, "lO")
+        less(0, "lA")
+        less(2, "lO")
+        less(3, "lA", "out")
+        vwait("sM")
+        less(1, "lO", "u", CW[p]["LW"], "resW")
+        less(2, "lB", "out")
+        less(0, "lB", "out")
+        less(1, "lC", "out", CW[p]["RW"], "resW")
         for q, eng, s_ in ((0, g.sync, sem.st0), (1, g.scalar, sem.st1)):
-            less(q * H, (q + 1) * H, ("lA", q * H, (q + 1) * H), "out")
-            eng.wait_ge(sem.dv, st["n"])
+            eng.wait_ge(sem.dv, done[q])
             eng.dma_start(T.y[:, q * H:(q + 1) * H], T.out[:, q * H:(q + 1) * H]).then_inc(s_, 16)
             eng.wait_ge(s_, 16)
 
     if i is not None:
         g.wait_ge(sem.sLd, 16)
-        for key in ("F1", "FW", "F3", "FS"):
+        for key in ("C1", "C2", "C3"):
             call(key)
     for key, cnt in marks:
         g.wait_ge(sem.dv, cnt)

from concourse.bass import DstId, RemoteDMATransfer
from concourse.mybir import AluOpType

B, Q, H, C = 64, 128, 256, 512

SCRATCH = {
    "xs": ("sbuf", [128, C], "float32"),
    "c15": ("sbuf", [128, C], "float32"),
    "wl": ("sbuf", [128, H], "float32"),
    "wl0": ("sbuf", [128, H], "float32"),
    "ll": ("sbuf", [128, H], "float32"),
    "rl": ("sbuf", [128, H], "float32"),
    "sc": ("sbuf", [128, 6 * B], "float32"),
    "sc0": ("sbuf", [128, 6 * B], "float32"),
    "ssum": ("sbuf", [128, H], "float32"),
    "m1": ("sbuf", [128, 3 * H], "float32"),
    "m2": ("sbuf", [128, 3 * H], "float32"),
    "part": ("sbuf", [128, H], "float32"),
    "res0": ("sbuf", [128, H], "float32"),
    "resL": ("sbuf", [128, H], "float32"),
    "resR": ("sbuf", [128, H], "float32"),
    "resW": ("sbuf", [128, H], "float32"),
    "lO": ("sbuf", [128, C], "float32"),
    "lA": ("sbuf", [128, C], "float32"),
    "lB": ("sbuf", [128, C], "float32"),
    "lC": ("sbuf", [128, C], "float32"),
    "out": ("sbuf", [128, C], "float32"),
    "wwp": ("psum", [128, C], "float32"),
    "llp": ("psum", [128, C], "float32"),
    "pm": ("psum", [128, C], "float32"),
    "ts": ("psum", [128, C], "float32"),
    "t1": ("psum", [128, C], "float32"),
    "t2": ("psum", [128, C], "float32"),
    "u": ("psum", [128, C], "float32"),
}
SEMAPHORES = ["sLd", "sL", "sR", "sW", "sW0", "sE", "sF", "sG", "sM", "sLoc", "dv", "st0", "st1"]


def _plan(T, topo):
    hosts = []
    for c in T.cores:
        if topo.host(c) not in hosts:
            hosts.append(topo.host(c))
    by = {h: [c for c in T.cores if topo.host(c) == h] for h in hosts}
    ring = [hosts[0]]
    while len(ring) < len(hosts):
        ring.append([h for h in hosts if h not in ring and topo.may_write(by[ring[-1]][0], by[h][0])][0])
    n = len(ring)
    ranks = [by[h] for h in ring]
    world = range((max(hosts) + 1) * topo.CORES_PER_HOST)
    CW, role = [], {}
    for p in range(n):
        r = ranks[p]
        others = [c for c in world if topo.host(c) == ring[p] and topo.chip(c) == topo.chip(r[0]) and c not in r]
        CW.append({"LW": r[0:2], "RW": r[2:4], 2: others[0:2], 3: others[2:4]})
        for k in CW[p]:
            for hb in (0, 1):
                role[CW[p][k][hb]] = {"p": p, "k": k, "hb": hb}
        for i in range(4):
            role[r[i]]["i"] = i
    sends = {}
    for p in range(n):
        rt, lf = (p + 1) % n, (p - 1) % n

        def blk(q, d, hb):
            return (2 * ((q + d) % n) + hb) * B

        def sl(name, i):
            return (name, i * B, (i + 1) * B)

        def xb(b):
            return ("xs", b, b + B)
        for i, c in enumerate(ranks[p]):
            F = {"C1": [], "C2": [], "C3": []}
            for hb in (0, 1):
                for d in (2, 3):
                    F["C1"].append((CW[rt][d][hb], sl("ll", i), xb(blk(rt, d, hb)), 1, "off", "sL"))
                    F["C1"].append((CW[lf][d][hb], sl("rl", i), xb(blk(lf, d, hb)), 1, "off", "sR"))
                    F["C1"].append((CW[p][d][hb], sl("wl", i), xb(blk(p, d, hb)), 2, "hi", "sW"))
                F["C2"].append((CW[rt]["LW"][hb], sl("ll", i), xb(blk(rt, 1, hb)), 2, "off", "sL"))
                F["C2"].append((CW[lf]["RW"][hb], sl("rl", i), xb(blk(lf, 1, hb)), 2, "off", "sR"))
                F["C2"].append((CW[p]["LW"][hb], sl("wl", i), xb(blk(p, 1, hb)), 2, "hi", "sW"))
                F["C2"].append((CW[p]["RW"][hb], sl("wl", i), xb(blk(p, 1, hb)), 2, "hi", "sW"))
                F["C3"].append((CW[p]["LW"][hb], sl("wl0", i), xb(blk(p, 0, hb)), 4, "hi", "sW0"))
            for key in F:
                sends[(c, key)] = [t for t in F[key] if t[0] != c]

        def ret(c, key, to, land, b, res, pool, sm):
            sends[(c, key)] = sends.get((c, key), []) + [
                (to[i], (land, b, b + B), sl(res, i), 2, pool, sm) for i in range(4) if to[i] != c]
        for hb in (0, 1):
            for d in (2, 3):
                c, b = CW[p][d][hb], blk(p, d, hb)
                ret(c, "RR", ranks[rt], "lA", b, "resR", "off", "sF")
                ret(c, "RX", ranks[lf], "lA", b, "resL", "off", "sG")
                ret(c, "RX", ranks[p], "lO", b, "resW", "hi", "sG")
            b = blk(p, 1, hb)
            ret(CW[p]["LW"][hb], "R0", ranks[p], "lO", blk(p, 0, hb), "res0", "hi", "sE")
            ret(CW[p]["LW"][hb], "RX", ranks[lf], "lB", b, "resL", "off", "sM")
            ret(CW[p]["LW"][hb], "RX", ranks[p], "lO", b, "resW", "hi", "sM")
            ret(CW[p]["RW"][hb], "RX", ranks[rt], "lB", b, "resR", "off", "sM")
            ret(CW[p]["RW"][hb], "RX", ranks[p], "lC", b, "resW", "hi", "sM")
    expect = {}
    for key in sends:
        for t in sends[key]:
            expect[(t[0], t[5])] = expect.get((t[0], t[5]), 0) + t[3]
    return role, sends, expect, ranks, CW, n


def rank_program(g, core, T, topo):
    if not [c for c in T.cores if topo.host(c) == topo.host(core) and topo.chip(c) == topo.chip(core)]:
        return
    role, sends, expect, ranks, CW, n = _plan(T, topo)
    me = role[core]
    p, kind, hb = me["p"], me["k"], me["hb"]
    i = me.get("i")
    v = g.vector
    sem = T.sem

    def ap(o):
        return T[o[0]][:, o[1]:o[2]]

    def bits(m):
        return [1 << e for e in range(16) if (m >> e) & 1]
    off = bits(topo.mask(core, ranks[(p + 1) % n][0]))
    on = bits(topo.mask(core, [c for c in role if role[c]["p"] == p and c != core][0]))
    pools = {"off": off, "hi": [e for e in on if e not in off]}
    loc = [0]

    def call(key):
        used = {"off": 0, "hi": 0}
        trs = []
        for (dst, d_, s_, ne, pool, sm) in sends[(core, key)]:
            m = sum(pools[pool][used[pool]:used[pool] + ne])
            used[pool] += ne
            rid, pid = topo.addr(dst, core)
            trs.append(RemoteDMATransfer(dst_ids=[DstId(rid=rid, pnc=pid)], dma_engine_mask=m, remote_sem=sem[sm],
                                         src=ap(s_), dst=ap(d_)))
            loc[0] += ne
        g.remote_dma_fused(trs, local_sem=sem.sLoc)

    st = {"n": 0, "w": 0}
    lastw, lastr = {}, {}

    def keys(o):
        return [(o[0], k) for k in range(o[1] // B, (o[2] + B - 1) // B)]

    def dep(reads, out):
        need = 0
        for o in reads + [out]:
            for k in keys(o):
                need = max(need, lastw.get(k, 0))
        for k in keys(out):
            need = max(need, lastr.get(k, 0))
        if need > st["w"]:
            v.wait_ge(sem.dv, need)
            st["w"] = need
        st["n"] += 1
        for o in reads:
            for k in keys(o):
                lastr[k] = st["n"]
        for k in keys(out):
            lastw[k] = st["n"]

    def tt(out, a, b, op):
        dep([a, b], out)
        v.tensor_tensor(out=ap(out), in0=ap(a), in1=ap(b), op=op).then_inc(sem.dv, 1)

    def cp(out, a):
        dep([a], out)
        v.tensor_copy(out=ap(out), in_=ap(a)).then_inc(sem.dv, 1)

    def vwait(name):
        if expect.get((core, name), 0):
            v.wait_ge(sem[name], expect[(core, name)])

    def sub(o, a, b):
        return (o[0], o[1] + a * B, o[1] + b * B)

    ADD, MIN, SUBT = AluOpType.add, AluOpType.min, AluOpType.subtract

    def wide(dst, src):
        cp((dst, 0, H), (src, 0, H))
        cp((dst, H, H + 3 * B), (src, 0, 3 * B))

    def inside(w, wp, s, ts, ss):
        c1, c2 = (s, 0, H), (s, H, H + 2 * B)
        tt(c1, (w, 0, H), (wp, B, B + H), MIN)
        tt(c2, (w, 0, 2 * B), (wp, 2 * B, 4 * B), MIN)
        tt(sub(ts, 1, 4), sub(c1, 1, 4), sub(c1, 0, 3), ADD)
        tt(sub(ts, 0, 1), sub(c1, 0, 1), sub(c1, 3, 4), ADD)
        tt(sub(ss, 2, 4), sub(ts, 2, 4), c2, ADD)
        tt(sub(ss, 0, 2), sub(ts, 0, 2), c2, ADD)

    def mins(A, Bp, M):
        for k in range(4):
            tt(M[k], (A, 0, H), (Bp, k * B, k * B + H), MIN)

    def sum_a(M, t, res):
        for k in (1, 2, 3):
            for h in (0, 2):
                tt(sub(res if k == 3 else t, h, h + 2), sub(M[0] if k == 1 else t, h, h + 2), sub(M[k], h, h + 2), ADD)

    def sum_b(M, t, res, part):
        if part:
            tt(t, M[0], part, ADD)
        for k in (1, 2, 3):
            base = M[0] if (k == 1 and not part) else t
            o = res if k == 3 else t
            tt(sub(o, k, 4), sub(base, k, 4), sub(M[k], 0, 4 - k), ADD)
            tt(sub(o, 0, k), sub(base, 0, k), sub(M[k], 4 - k, 4), ADD)

    marks = []

    def mark(key):
        marks.append((key, st["n"]))

    def col(dd):
        return ((p + dd) % n) * Q

    M1 = [("pm", 0, H)] + [("m1", k * H, (k + 1) * H) for k in range(3)]
    M2 = [("pm", H, C)] + [("m2", k * H, (k + 1) * H) for k in range(3)]
    ss = ("ssum", 0, H)

    if i is not None:
        g.sync.dma_start(T.xs[:], T.x[:]).then_inc(sem.sLd, 16)
        dep([], ("c15", 0, C))
        v.memset(T.c15[:], float(len(T.cores) - 1)).then_inc(sem.dv, 1)
        v.wait_ge(sem.sLd, 16)
        b1 = col(1) + hb * B
        cp(("wl", i * B, (i + 1) * B), ("xs", b1, b1 + B))
        if kind == "LW":
            cp(("wl0", i * B, (i + 1) * B), ("xs", col(0) + hb * B, col(0) + hb * B + B))
        tt(("u", 0, C), ("xs", 0, C), ("c15", 0, C), AluOpType.mult)

    if kind == "LW":
        vwait("sW")
        wide("wwp", "wl")
        inside("wl", "wwp", "sc", ("ts", 0, H), ss)
        vwait("sW0")
        wide("llp", "wl0")
        inside("wl0", "llp", "sc0", ("ts", H, C), ("res0", 0, H))
        mark("R0")
        vwait("sL")
        mins("ll", "wwp", M1)
        sum_a(M1, ("t1", 0, H), ("resL", 0, H))
        sum_b(M1, ("t1", H, C), ("resW", 0, H), ss)
        mark("RX")
    elif kind == "RW":
        vwait("sW")
        wide("wwp", "wl")
        vwait("sR")
        mins("rl", "wwp", M2)
        sum_a(M2, ("t2", 0, H), ("resR", 0, H))
        sum_b(M2, ("t2", H, C), ("resW", 0, H), None)
        mark("RX")
    else:
        vwait("sW")
        wide("wwp", "wl")
        inside("wl", "wwp", "sc", ("ts", 0, H), ss)
        vwait("sL")
        wide("llp", "ll")
        vwait("sR")
        mins("rl", "llp", M2)
        sum_a(M2, ("t2", 0, H), ("resR", 0, H))
        mark("RR")
        mins("ll", "wwp", M1)
        sum_b(M1, ("t1", H, C), ("resW", 0, H), ss)
        sum_a(M1, ("t1", 0, H), ("part", 0, H))
        sum_b(M2, ("t2", H, C), ("resL", 0, H), ("part", 0, H))
        mark("RX")

    if i is not None:
        done = {}

        def less(dd, land, o="u", makers=None, res=None):
            if makers and core in makers:
                for h in (0, 1):
                    c0 = col(dd) + h * B
                    tt((o, c0, c0 + B), ("u", c0, c0 + B),
                       (res, i * B, (i + 1) * B) if makers[h] == core else (land, c0, c0 + B), SUBT)
            else:
                tt((o, col(dd), col(dd) + Q), ("u", col(dd), col(dd) + Q), (land, col(dd), col(dd) + Q), SUBT)
            if o == "out":
                done[col(dd) // H] = st["n"]
        vwait("sE")
        less(0, "lO", "u", CW[p]["LW"], "res0")
        vwait("sF")
        less(1, "lA")
        less(2, "lA")
        vwait("sG")
        less(3, "lO")
        less(0, "lA")
        less(2, "lO")
        less(3, "lA", "out")
        vwait("sM")
        less(1, "lO", "u", CW[p]["LW"], "resW")
        less(2, "lB", "out")
        less(0, "lB", "out")
        less(1, "lC", "out", CW[p]["RW"], "resW")
        for q, eng, s_ in ((0, g.sync, sem.st0), (1, g.scalar, sem.st1)):
            eng.wait_ge(sem.dv, done[q])
            eng.dma_start(T.y[:, q * H:(q + 1) * H], T.out[:, q * H:(q + 1) * H]).then_inc(s_, 16)
            eng.wait_ge(s_, 16)

    if i is not None:
        g.wait_ge(sem.sLd, 16)
        for key in ("C1", "C2", "C3"):
            call(key)
    for key, cnt in marks:
        g.wait_ge(sem.dv, cnt)
        call(key)
    g.wait_ge(sem.sLoc, loc[0])
    g.wait_ge(sem.dv, st["n"])
